import numpy as np
import ml_dtypes


def mxq(x, axis, fmt="e4m3"):
    dtype, down = {"e4m3": (ml_dtypes.float8_e4m3fn, 7), "e5m2": (ml_dtypes.float8_e5m2, 14)}[fmt]
    v = np.moveaxis(np.asarray(x, np.float32).astype(ml_dtypes.bfloat16).astype(np.float64), axis, -1)
    blocks = v.reshape(v.shape[:-1] + (-1, 32))
    amax = np.abs(blocks).max(-1, keepdims=True)
    byte = np.maximum(np.where(amax > 0, np.frexp(amax)[1] - 1 + 127, 0) - down, 1)
    scale = np.exp2(byte - 127.0)
    codes = (blocks / scale).astype(np.float32).astype(dtype).astype(np.float64)
    return np.moveaxis((codes * scale).reshape(v.shape), -1, axis)


WIDE = False


def mx_kscale(k):
    if not WIDE:
        return np.ones(k)
    levels = np.array([10, -10, 5, -5, 0])
    if k % 512:
        return np.exp2(np.random.permutation(np.resize(levels, k // 32))).repeat(32)
    a = np.empty((k // 512, 16))
    for p in range(k // 512):
        a[p, :8] = np.random.permutation(np.resize(levels, 8))
        for g in range(8):
            far = levels[np.abs(levels - a[p, g]) >= 10]
            a[p, g + 8] = far[np.random.randint(len(far))]
    return np.exp2(a.ravel()).repeat(32)


def f64(x):
    return np.asarray(x).astype(np.float64)


def striped(idx):
    return np.tile(idx.reshape(-1, 16).T, (8, 1)).astype(np.uint16)


def unstriped(offs):
    return offs[:16].T.reshape(-1).astype(np.int64)


E2M1 = np.array([0.0, 0.5, 1.0, 1.5, 2.0, 3.0, 4.0, 6.0, -0.0, -0.5, -1.0, -1.5, -2.0, -3.0, -4.0, -6.0])


def pack_weight(w, fmt):
    k, n = w.shape
    w = f64(np.asarray(w, np.float32).astype(ml_dtypes.bfloat16)).reshape(k // 32, 32, n)
    amax = np.abs(w).max(1)
    if fmt == "e4m3":
        byte = np.frexp(amax)[1] - 1 + 127 - 7
    else:
        mant, ex = np.frexp(amax / 6.0)
        byte = np.where(mant > 0.5, ex, ex - 1) + 127
    byte = np.clip(np.where(amax > 0, byte, 1), 1, 254)
    scaled = (w * np.exp2(127.0 - byte)[:, None, :]).reshape(k, n).astype(np.float32)
    by_word = np.ascontiguousarray(scaled.reshape(k // 512, 128, 4, n).transpose(0, 1, 3, 2))
    if fmt == "e4m3":
        words = by_word.astype(ml_dtypes.float8_e4m3fn).view(np.uint8)
    else:
        c = by_word.astype(ml_dtypes.float4_e2m1fn).view(np.uint8) & 0xF
        words = (c[..., 0::2] | (c[..., 1::2] << 4)).reshape(k // 512, 128, 2 * n)
    return np.ascontiguousarray(words), np.ascontiguousarray(byte.astype(np.uint8).reshape(k // 512, 16, n))


def unpack_weight(words, scales, fmt):
    g, _, n = scales.shape
    words = np.ascontiguousarray(words).reshape(g, 128, n, -1)
    if fmt == "e4m3":
        vals = words.view(ml_dtypes.float8_e4m3fn).astype(np.float64)
    else:
        nib = np.empty((g, 128, n, 4), np.uint8)
        nib[..., 0::2] = words & 0xF
        nib[..., 1::2] = words >> 4
        vals = E2M1[nib]
    vals = vals * np.repeat(np.exp2(scales.astype(np.float64) - 127.0), 8, axis=1)[..., None]
    return vals.transpose(0, 1, 3, 2).reshape(g * 512, n)


def gelu(v):
    return 0.5 * v * (1.0 + np.tanh(np.sqrt(2.0 / np.pi) * (v + 0.044715 * v**3)))


def striped8(idx):
    return np.concatenate([v.reshape(-1, 16).T for v in idx]).astype(np.uint16)


def unstriped8(offs):
    return np.stack([offs[16 * g:16 * g + 16].T.reshape(-1) for g in range(8)]).astype(np.int64)


def heads(h, wgt, idx8):
    r = np.arange(h.shape[0])
    return wgt[r // 4 % 128] * h[r[:, None], idx8[r % 512 // 64]]


def put_heads(h, wgs, idx8, t2):
    r = np.arange(h.shape[0])
    page = np.zeros((h.shape[0], t2))
    page[r[:, None], idx8[r % 512 // 64]] = wgs[r // 4 % 128] * h
    return page


K, H, N, T, S, P, T2 = 1536, 1024, 512, 4096, 1024, 512, 1024

def setup_inputs():
    n = np.random.standard_normal
    s = mx_kscale(K)[:, None]
    u = mx_kscale(H)[:, None]
    d = {}
    d["tab_words"], d["tab_scales"] = pack_weight(n((K, T)) * s, "e4m3")
    d["offs"] = striped(np.random.permutation(T)[:S])
    d["w1"] = (n((K, H)) / K ** 0.5 / s).astype(np.float32)
    d["gain"] = (2.0 * np.exp(0.8 * n(H))).astype(np.float32)
    d["offs2"] = striped8(np.stack([np.random.permutation(S)[:P] for _ in range(8)]))
    d["wgt"] = np.repeat(np.random.uniform(0.5, 2.0, (8, P)), 16, axis=0).astype(np.float32)
    d["sens"] = (np.exp(0.3 * n(H)) * u[:, 0]).astype(np.float32)
    d["w2_words"], d["w2_scales"] = pack_weight(n((H, N)) / H ** 0.5 / u, "e2m1")
    d["thick"] = np.exp(0.4 * n((N, P))).astype(np.float32)
    d["wgo"] = np.repeat(np.random.uniform(0.5, 2.0, (8, P)), 16, axis=0).astype(np.float32)
    d["offs3"] = striped8(np.stack([np.random.permutation(T2)[:P] for _ in range(8)]))
    return d

def reference(tab_words, tab_scales, offs, w1, gain, offs2, wgt, sens, w2_words, w2_scales, thick, wgo, offs3):
    v = unpack_weight(tab_words, tab_scales, "e4m3")[:, unstriped(offs)]
    h = f64(gain)[:, None] * (mxq(f64(w1), 0, "e4m3").T @ v)
    x = heads(h, f64(wgt), unstriped8(offs2))
    z = np.sqrt(np.abs(x) + 1.0) * f64(sens)[:, None]
    w2 = unpack_weight(w2_words, w2_scales, "e2m1")
    y = f64(thick) * (w2.T @ mxq(z, 0, "e4m3"))
    return put_heads(y, f64(wgo), unstriped8(offs3), T2)

@@ -1,0 +1,213 @@
+from contextlib import ExitStack
+
+import concourse.mybir as mybir
+
+K, H, N, T, S, M, T2 = 1536, 1024, 512, 4096, 1024, 512, 1024
+FLOPS = 2 * K * H * S + 2 * H * N * M
+
+F32 = mybir.dt.float32
+BF16 = mybir.dt.bfloat16
+I32 = mybir.dt.int32
+U32 = mybir.dt.uint32
+U16 = mybir.dt.uint16
+U8 = mybir.dt.uint8
+FP8X4 = mybir.dt.float8_e4m3fn_x4
+FP4X4 = mybir.dt.float4_e2m1fn_x4
+ALU = mybir.AluOpType
+ACT = mybir.ActivationFunctionType
+
+P = 128
+PACK = 4
+PASS = P * PACK
+K_PASSES = K // PASS
+H_PASSES = H // PASS
+BANK = 512
+QUARTER = 128
+PARTS = ((0, 128), (128, 256), (256, 512))
+CAST_SPLIT = 88
+
+
+def tile_list_hide_defect_verdicts_kernel(
+    tc, tab_words, tab_scales, offs, w1, gain, offs2, wgt, sens, w2_words, w2_scales, thick, wgo, offs3, out
+):
+    nc = tc.nc
+    with ExitStack() as ctx:
+        keep = ctx.enter_context(tc.tile_pool(name="keep", bufs=1))
+        ring = ctx.enter_context(tc.tile_pool(name="ring", bufs=3))
+        hpool = ctx.enter_context(tc.tile_pool(name="hpool", bufs=4))
+        psum = ctx.enter_context(tc.psum_pool(name="psum", bufs=8))
+
+        strips = keep.tile([P, S // 16], U16, name="strips")
+        picks = keep.tile([P, M // 16], U16, name="picks")
+        places = keep.tile([P, M // 16], U16, name="places")
+        table = [keep.tile([P, T], I32, name="table%d" % a) for a in range(K_PASSES)]
+        table_scales = keep.tile([P, T], U8, name="table_scales")
+        w2_raw = keep.tile([P, H_PASSES, 2 * N], U8, name="w2_raw")
+        w2_raw_scales = keep.tile([P, H_PASSES, N], U8, name="w2_raw_scales")
+        w1_raw = [
+            [keep.tile([P, PACK, PASS], F32, name="w1_raw%d%d" % (b, a)) for a in range(K_PASSES)]
+            for b in range(H_PASSES)
+        ]
+        gains = keep.tile([P, H_PASSES, PACK], F32, name="gains")
+        senses = keep.tile([P, H_PASSES, PACK], F32, name="senses")
+        pick_weight = keep.tile([P, M], F32, name="pick_weight")
+        place_weight = keep.tile([P, M], F32, name="place_weight")
+        verdict = keep.tile([P, PACK, M], F32, name="verdict")
+        pages = [keep.tile([P, T2], F32, name="page%d" % i) for i in range(PACK)]
+
+        nc.vector.memset(table_scales[:].bitcast(I32), 0)
+        nc.vector.memset(w2_raw_scales[:].rearrange("p b c -> p (b c)").bitcast(I32), 0)
+        ones = keep.tile([P, 1], F32, name="ones")
+        one = keep.tile([P, 1], F32, name="one")
+        nc.vector.memset(ones[:], 1.0)
+        nc.scalar.activation(one[:], ones[:], ACT.Sqrt)
+
+        def load_table(a):
+            nc.sync.dma_start(table[a][:], tab_words[a].rearrange("p t i -> p (t i)").bitcast(I32))
+
+        def load_w1(b, a):
+            rows = w1[a * PASS : (a + 1) * PASS, b * PASS : (b + 1) * PASS]
+            nc.sync.dma_start(w1_raw[b][a][:], rows.rearrange("(p j) c -> p j c", j=PACK))
+
+        nc.sync.dma_start(strips[:], offs)
+        load_table(0)
+        load_table(1)
+        nc.sync.dma_start(w2_raw[:].bitcast(I32), w2_words.rearrange("b p c -> p b c").bitcast(I32))
+        load_table(2)
+        for a in range(K_PASSES):
+            load_w1(0, a)
+        nc.sync.dma_start(pick_weight[:], wgt)
+        nc.sync.dma_start(gains[:], gain.rearrange("(b p i) -> p b i", b=H_PASSES, i=PACK))
+        nc.sync.dma_start(picks[:], offs2)
+        nc.sync.dma_start(senses[:], sens.rearrange("(b p i) -> p b i", b=H_PASSES, i=PACK))
+        for a in range(K_PASSES):
+            load_w1(1, a)
+        nc.sync.dma_start(verdict[:], thick.rearrange("(p i) m -> p i m", i=PACK))
+        nc.sync.dma_start(place_weight[:], wgo)
+        nc.sync.dma_start(places[:], offs3)
+
+        for quad in range(4):
+            nc.gpsimd.dma_start(
+                table_scales[32 * quad : 32 * quad + 4 * K_PASSES, :].bitcast(I32),
+                tab_scales[:, 4 * quad : 4 * quad + 4, :].bitcast(I32),
+            )
+        for quad in range(4):
+            nc.gpsimd.dma_start(
+                w2_raw_scales[32 * quad : 32 * quad + 4, :, :].bitcast(I32),
+                w2_scales[:, 4 * quad : 4 * quad + 4, :].rearrange("b r c -> r b c").bitcast(I32),
+            )
+
+        for page in pages:
+            nc.vector.memset(page[:], 0.0)
+
+        strip_codes = [keep.tile([P, S], U32, name="strip_codes%d" % a, align_bytes=64) for a in range(K_PASSES)]
+        strip_scales = keep.tile([P, S], U8, name="strip_scales", align_bytes=64)
+        for a in range(K_PASSES):
+            nc.vector.tensor_copy(strip_codes[a][:], table[a][:].bitcast(U32).indirect(strips[:]))
+        nc.vector.tensor_copy(strip_scales[:], table_scales[:].indirect(strips[:]))
+
+        w2_codes = keep.tile([P, H_PASSES, PACK, 2 * P], U8, name="w2_codes", align_bytes=64)
+        w2_planes = keep.tile([P, H_PASSES, PACK, P], U8, name="w2_planes", align_bytes=64)
+        nc.vector.tensor_copy(
+            w2_codes[:].rearrange("p b i (q e) -> p b i q e", e=2),
+            w2_raw[:].rearrange("p b (q i e) -> p b i q e", i=PACK, e=2),
+        )
+        nc.vector.tensor_copy(w2_planes[:], w2_raw_scales[:].rearrange("p b (q i) -> p b i q", i=PACK))
+
+        pick_size = keep.tile([P, M], F32, name="pick_size")
+        picked = [keep.tile([P, PACK, M], F32, name="picked%d" % b) for b in range(H_PASSES)]
+
+        for b in range(H_PASSES):
+            banks = [[psum.tile([P, BANK], F32, name="bank", tag="bank") for half in range(2)] for i in range(PACK)]
+            for a in range(K_PASSES):
+                grouped = ring.tile([P, PACK, P, PACK], BF16, name="grouped", align_bytes=64)
+                dst = grouped[:].rearrange("p i q j -> p q j i")
+                src = w1_raw[b][a][:].rearrange("p j (q i) -> p q j i", i=PACK)
+                split = {(1, 0): P, (1, 1): 0}.get((b, a), CAST_SPLIT)
+                if split > 0:
+                    nc.vector.tensor_copy(dst[:, :split], src[:, :split])
+                if split < P:
+                    nc.scalar.copy(dst[:, split:], src[:, split:])
+                codes = keep.tile([P, PASS], U32, name="w1_codes%d%d" % (b, a), align_bytes=64)
+                scales = keep.tile([P, PASS], U8, name="w1_scales%d%d" % (b, a), align_bytes=64)
+                nc.vector.quantize_mx(
+                    out=codes[:].bitcast(FP8X4), scales=scales[:], in_=grouped[:].rearrange("p i q j -> p (i q j)")
+                )
+                for i in range(PACK):
+                    for half in range(2):
+                        cols = slice(half * BANK, (half + 1) * BANK)
+                        nc.tensor.matmul_mx(
+                            out=banks[i][half][:],
+                            lhsT=codes[:, i * P : (i + 1) * P].bitcast(FP8X4),
+                            lhsT_scale=scales[:, i * P : (i + 1) * P],
+                            rhs=strip_codes[a][:, cols].bitcast(FP8X4),
+                            rhs_scale=strip_scales[4 * a : P, cols],
+                            start=(a == 0),
+                            stop=(a == K_PASSES - 1),
+                        )
+            if b == 0:
+                nc.vector.scalar_tensor_tensor(
+                    pick_size[:], pick_weight[:], -1.0, pick_weight[:], op0=ALU.mult, op1=ALU.max
+                )
+            for i in range(PACK):
+                size = hpool.tile([P, S], F32, name="size")
+                for half in range(2):
+                    nc.scalar.activation(
+                        size[:, half * BANK : (half + 1) * BANK],
+                        banks[i][half][:],
+                        ACT.Abs,
+                        scale=gains[:, b, i : i + 1],
+                    )
+                nc.vector.tensor_tensor(picked[b][:, i, :], size[:].indirect(picks[:]), pick_size[:], ALU.mult)
+
+        rows = out.rearrange("(p i) t -> p i t", i=PACK)
+        for c0, c1 in PARTS:
+            width = c1 - c0
+            z_codes, z_scales = [], []
+            for b in range(H_PASSES):
+                planes = keep.tile([P, PACK, width], BF16, name="planes%d_%d" % (b, c0))
+                if c0 > 0:
+                    nc.scalar.activation(picked[b][:, :, c0:c1], picked[b][:, :, c0:c1], ACT.Sqrt, bias=one[:])
+                for i in range(PACK):
+                    if c0 == 0:
+                        nc.scalar.activation(picked[b][:, i, c0:c1], picked[b][:, i, c0:c1], ACT.Sqrt, bias=one[:])
+                    nc.scalar.activation(
+                        planes[:, i, :], picked[b][:, i, c0:c1], ACT.Copy, scale=senses[:, b, i : i + 1]
+                    )
+                woven = keep.tile([P, width, PACK], BF16, name="woven%d_%d" % (b, c0), align_bytes=64)
+                nc.vector.tensor_copy(
+                    woven[:].rearrange("p (c e) i -> p c i e", e=4),
+                    planes[:].rearrange("p i (c e) -> p c i e", e=4),
+                )
+                codes = keep.tile([P, width], U32, name="z_codes%d_%d" % (b, c0), align_bytes=64)
+                scales = keep.tile([P, width], U8, name="z_scales%d_%d" % (b, c0), align_bytes=64)
+                nc.vector.quantize_mx(
+                    out=codes[:].bitcast(FP8X4), scales=scales[:], in_=woven[:].rearrange("p m i -> p (m i)")
+                )
+                z_codes.append(codes)
+                z_scales.append(scales)
+            for m0 in range(c0, c1, QUARTER):
+                bank = psum.tile([P, PACK, QUARTER], F32, name="sums", tag="bank")
+                cols = slice(m0 - c0, m0 - c0 + QUARTER)
+                for i in range(PACK):
+                    for b in range(H_PASSES):
+                        nc.tensor.matmul_mx(
+                            out=bank[:, i, :],
+                            lhsT=w2_codes[:, b, i, :].bitcast(FP4X4),
+                            lhsT_scale=w2_planes[:, b, i, :],
+                            rhs=z_codes[b][:, cols].bitcast(FP8X4),
+                            rhs_scale=z_scales[b][:, cols],
+                            start=(b == 0),
+                            stop=(b == H_PASSES - 1),
+                        )
+                part = verdict[:, :, m0 : m0 + QUARTER]
+                nc.vector.tensor_tensor(part, bank[:], part, ALU.mult)
+            for i in range(PACK):
+                nc.vector.tensor_tensor(
+                    pages[i][:].indirect(places[:, c0 // 16 : c1 // 16]),
+                    verdict[:, i, c0:c1],
+                    place_weight[:, c0:c1],
+                    ALU.mult,
+                )
+                if c1 == M:
+                    nc.sync.dma_start(rows[:, i, :], pages[i][:])

@@ -23,7 +23,6 @@ K_PASSES = K // PASS
 H_PASSES = H // PASS
 BANK = 512
 QUARTER = 128
-PARTS = ((0, 128), (128, 256), (256, 512))
 CAST_SPLIT = 88
 
 
@@ -34,7 +33,7 @@ def tile_list_hide_defect_verdicts_kernel(
     with ExitStack() as ctx:
         keep = ctx.enter_context(tc.tile_pool(name="keep", bufs=1))
         ring = ctx.enter_context(tc.tile_pool(name="ring", bufs=3))
-        hpool = ctx.enter_context(tc.tile_pool(name="hpool", bufs=4))
+        hpool = ctx.enter_context(tc.tile_pool(name="hpool", bufs=6))
         psum = ctx.enter_context(tc.psum_pool(name="psum", bufs=8))
 
         strips = keep.tile([P, S // 16], U16, name="strips")
@@ -45,14 +44,14 @@ def tile_list_hide_defect_verdicts_kernel(
         w2_raw = keep.tile([P, H_PASSES, 2 * N], U8, name="w2_raw")
         w2_raw_scales = keep.tile([P, H_PASSES, N], U8, name="w2_raw_scales")
         w1_raw = [
-            [keep.tile([P, PACK, PASS], F32, name="w1_raw%d%d" % (b, a)) for a in range(K_PASSES)]
+            [keep.tile([P, PACK, PASS], F32, name="w1_raw", tag="w1_raw%d%d" % (b, a)) for a in range(K_PASSES)]
             for b in range(H_PASSES)
         ]
         gains = keep.tile([P, H_PASSES, PACK], F32, name="gains")
         senses = keep.tile([P, H_PASSES, PACK], F32, name="senses")
         pick_weight = keep.tile([P, M], F32, name="pick_weight")
         place_weight = keep.tile([P, M], F32, name="place_weight")
-        verdict = keep.tile([P, PACK, M], F32, name="verdict")
+        thickness = keep.tile([P, PACK, M], F32, name="thickness")
         pages = [keep.tile([P, T2], F32, name="page%d" % i) for i in range(PACK)]
 
         nc.vector.memset(table_scales[:].bitcast(I32), 0)
@@ -71,8 +70,18 @@ def tile_list_hide_defect_verdicts_kernel(
 
         nc.sync.dma_start(strips[:], offs)
         load_table(0)
+        for quad in range(4):
+            nc.sync.dma_start(
+                table_scales[32 * quad : 32 * quad + 4 * K_PASSES, :].bitcast(I32),
+                tab_scales[:, 4 * quad : 4 * quad + 4, :].bitcast(I32),
+            )
         load_table(1)
         nc.sync.dma_start(w2_raw[:].bitcast(I32), w2_words.rearrange("b p c -> p b c").bitcast(I32))
+        for quad in range(4):
+            nc.sync.dma_start(
+                w2_raw_scales[32 * quad : 32 * quad + 4, :, :].bitcast(I32),
+                w2_scales[:, 4 * quad : 4 * quad + 4, :].rearrange("b r c -> r b c").bitcast(I32),
+            )
         load_table(2)
         for a in range(K_PASSES):
             load_w1(0, a)
@@ -82,20 +91,9 @@ def tile_list_hide_defect_verdicts_kernel(
         nc.sync.dma_start(senses[:], sens.rearrange("(b p i) -> p b i", b=H_PASSES, i=PACK))
         for a in range(K_PASSES):
             load_w1(1, a)
-        nc.sync.dma_start(verdict[:], thick.rearrange("(p i) m -> p i m", i=PACK))
+        nc.sync.dma_start(thickness[:], thick.rearrange("(p i) m -> p i m", i=PACK))
         nc.sync.dma_start(place_weight[:], wgo)
         nc.sync.dma_start(places[:], offs3)
-
-        for quad in range(4):
-            nc.gpsimd.dma_start(
-                table_scales[32 * quad : 32 * quad + 4 * K_PASSES, :].bitcast(I32),
-                tab_scales[:, 4 * quad : 4 * quad + 4, :].bitcast(I32),
-            )
-        for quad in range(4):
-            nc.gpsimd.dma_start(
-                w2_raw_scales[32 * quad : 32 * quad + 4, :, :].bitcast(I32),
-                w2_scales[:, 4 * quad : 4 * quad + 4, :].rearrange("b r c -> r b c").bitcast(I32),
-            )
 
         for page in pages:
             nc.vector.memset(page[:], 0.0)
@@ -115,17 +113,15 @@ def tile_list_hide_defect_verdicts_kernel(
         nc.vector.tensor_copy(w2_planes[:], w2_raw_scales[:].rearrange("p b (q i) -> p b i q", i=PACK))
 
         pick_size = keep.tile([P, M], F32, name="pick_size")
-        picked = [keep.tile([P, PACK, M], F32, name="picked%d" % b) for b in range(H_PASSES)]
 
-        for b in range(H_PASSES):
+        def first_product(b):
             banks = [[psum.tile([P, BANK], F32, name="bank", tag="bank") for half in range(2)] for i in range(PACK)]
             for a in range(K_PASSES):
                 grouped = ring.tile([P, PACK, P, PACK], BF16, name="grouped", align_bytes=64)
                 dst = grouped[:].rearrange("p i q j -> p q j i")
                 src = w1_raw[b][a][:].rearrange("p j (q i) -> p q j i", i=PACK)
-                split = {(1, 0): P, (1, 1): 0}.get((b, a), CAST_SPLIT)
-                if split > 0:
-                    nc.vector.tensor_copy(dst[:, :split], src[:, :split])
+                split = P if b == 1 and a < K_PASSES - 1 else CAST_SPLIT
+                nc.vector.tensor_copy(dst[:, :split], src[:, :split])
                 if split < P:
                     nc.scalar.copy(dst[:, split:], src[:, split:])
                 codes = keep.tile([P, PASS], U32, name="w1_codes%d%d" % (b, a), align_bytes=64)
@@ -145,69 +141,118 @@ def tile_list_hide_defect_verdicts_kernel(
                             start=(a == 0),
                             stop=(a == K_PASSES - 1),
                         )
-            if b == 0:
-                nc.vector.scalar_tensor_tensor(
-                    pick_size[:], pick_weight[:], -1.0, pick_weight[:], op0=ALU.mult, op1=ALU.max
+            return banks
+
+        def response_size(b, i, banks):
+            size = hpool.tile([P, S], F32, name="size")
+            for half in range(2):
+                nc.scalar.activation(
+                    size[:, half * BANK : (half + 1) * BANK], banks[i][half][:], ACT.Abs, scale=gains[:, b, i : i + 1]
                 )
+            return size
+
+        def pick(dst, size, c0, c1):
+            nc.vector.tensor_tensor(dst, size[:].indirect(picks[:, c0 // 16 : c1 // 16]), pick_size[:, c0:c1], ALU.mult)
+
+        def compress(b, c0, c1, groups, weaver, tag):
+            width = c1 - c0
+            planes = keep.tile([P, PACK, width], BF16, name="planes%d_%d" % (b, c0))
+            i = 0
+            for group in groups:
+                nc.scalar.activation(group, group, ACT.Sqrt, bias=one[:])
+                for g in range(group.shape[1]):
+                    nc.scalar.activation(planes[:, i, :], group[:, g, :], ACT.Copy, scale=senses[:, b, i : i + 1])
+                    i = i + 1
+            woven = keep.tile([P, width, PACK], BF16, name="woven", tag=tag, align_bytes=64)
+            weaver(
+                woven[:].rearrange("p (c e) i -> p c i e", e=4),
+                planes[:].rearrange("p i (c e) -> p c i e", e=4),
+            )
+            codes = keep.tile([P, width], U32, name="z_codes%d_%d" % (b, c0), align_bytes=64)
+            scales = keep.tile([P, width], U8, name="z_scales%d_%d" % (b, c0), align_bytes=64)
+            nc.vector.quantize_mx(
+                out=codes[:].bitcast(FP8X4), scales=scales[:], in_=woven[:].rearrange("p m i -> p (m i)")
+            )
+            return codes, scales
+
+        def second_product(z):
+            bank = psum.tile([P, PACK, QUARTER], F32, name="sums", tag="bank")
             for i in range(PACK):
-                size = hpool.tile([P, S], F32, name="size")
-                for half in range(2):
-                    nc.scalar.activation(
-                        size[:, half * BANK : (half + 1) * BANK],
-                        banks[i][half][:],
-                        ACT.Abs,
-                        scale=gains[:, b, i : i + 1],
+                for b in range(H_PASSES):
+                    nc.tensor.matmul_mx(
+                        out=bank[:, i, :],
+                        lhsT=w2_codes[:, b, i, :].bitcast(FP4X4),
+                        lhsT_scale=w2_planes[:, b, i, :],
+                        rhs=z[b][0][:].bitcast(FP8X4),
+                        rhs_scale=z[b][1][:],
+                        start=(b == 0),
+                        stop=(b == H_PASSES - 1),
                     )
-                nc.vector.tensor_tensor(picked[b][:, i, :], size[:].indirect(picks[:]), pick_size[:], ALU.mult)
+            return bank
 
         rows = out.rearrange("(p i) t -> p i t", i=PACK)
-        for c0, c1 in PARTS:
-            width = c1 - c0
-            z_codes, z_scales = [], []
-            for b in range(H_PASSES):
-                planes = keep.tile([P, PACK, width], BF16, name="planes%d_%d" % (b, c0))
-                if c0 > 0:
-                    nc.scalar.activation(picked[b][:, :, c0:c1], picked[b][:, :, c0:c1], ACT.Sqrt, bias=one[:])
-                for i in range(PACK):
-                    if c0 == 0:
-                        nc.scalar.activation(picked[b][:, i, c0:c1], picked[b][:, i, c0:c1], ACT.Sqrt, bias=one[:])
-                    nc.scalar.activation(
-                        planes[:, i, :], picked[b][:, i, c0:c1], ACT.Copy, scale=senses[:, b, i : i + 1]
-                    )
-                woven = keep.tile([P, width, PACK], BF16, name="woven%d_%d" % (b, c0), align_bytes=64)
-                nc.vector.tensor_copy(
-                    woven[:].rearrange("p (c e) i -> p c i e", e=4),
-                    planes[:].rearrange("p i (c e) -> p c i e", e=4),
-                )
-                codes = keep.tile([P, width], U32, name="z_codes%d_%d" % (b, c0), align_bytes=64)
-                scales = keep.tile([P, width], U8, name="z_scales%d_%d" % (b, c0), align_bytes=64)
-                nc.vector.quantize_mx(
-                    out=codes[:].bitcast(FP8X4), scales=scales[:], in_=woven[:].rearrange("p m i -> p (m i)")
-                )
-                z_codes.append(codes)
-                z_scales.append(scales)
-            for m0 in range(c0, c1, QUARTER):
-                bank = psum.tile([P, PACK, QUARTER], F32, name="sums", tag="bank")
-                cols = slice(m0 - c0, m0 - c0 + QUARTER)
-                for i in range(PACK):
-                    for b in range(H_PASSES):
-                        nc.tensor.matmul_mx(
-                            out=bank[:, i, :],
-                            lhsT=w2_codes[:, b, i, :].bitcast(FP4X4),
-                            lhsT_scale=w2_planes[:, b, i, :],
-                            rhs=z_codes[b][:, cols].bitcast(FP8X4),
-                            rhs_scale=z_scales[b][:, cols],
-                            start=(b == 0),
-                            stop=(b == H_PASSES - 1),
-                        )
-                part = verdict[:, :, m0 : m0 + QUARTER]
-                nc.vector.tensor_tensor(part, bank[:], part, ALU.mult)
-            for i in range(PACK):
-                nc.vector.tensor_tensor(
-                    pages[i][:].indirect(places[:, c0 // 16 : c1 // 16]),
-                    verdict[:, i, c0:c1],
-                    place_weight[:, c0:c1],
-                    ALU.mult,
-                )
-                if c1 == M:
-                    nc.sync.dma_start(rows[:, i, :], pages[i][:])
+
+        def thicken(verdict, bank, i0, i1, c0):
+            nc.vector.tensor_tensor(verdict, bank[:, i0:i1, :], thickness[:, i0:i1, c0 : c0 + QUARTER], ALU.mult)
+
+        def place(verdict, i, c0, c1):
+            nc.vector.tensor_tensor(
+                pages[i][:].indirect(places[:, c0 // 16 : c1 // 16]), verdict, place_weight[:, c0:c1], ALU.mult
+            )
+            if c1 == M:
+                nc.sync.dma_start(rows[:, i, :], pages[i][:])
+
+        def place_pair(bank, i0, c0, tag):
+            verdict = keep.tile([P, 2, QUARTER], F32, name="verdict", tag=tag, align_bytes=64)
+            thicken(verdict[:], bank, i0, i0 + 2, c0)
+            for i in range(2):
+                place(verdict[:, i, :], i0 + i, c0, c0 + QUARTER)
+
+        banks0 = first_product(0)
+        nc.scalar.activation(pick_size[:], pick_weight[:], ACT.Abs)
+        sizes0 = [response_size(0, i, banks0) for i in range(PACK)]
+        banks1 = first_product(1)
+        early = keep.tile([P, 1, M], F32, name="early")
+        late = keep.tile([P, PACK - 1, M], F32, name="late", tag="w1_raw12")
+        pick(early[:, 0, :], sizes0[0], 0, M)
+        for i in range(1, PACK):
+            pick(late[:, i - 1, :], sizes0[i], 0, M)
+        head = keep.tile([P, PACK, QUARTER], F32, name="head")
+        sizes1 = []
+        for i in range(PACK):
+            sizes1.append(response_size(1, i, banks1))
+            pick(head[:, i, :], sizes1[i], 0, QUARTER)
+
+        c0, c1 = 0, QUARTER
+        z = [
+            compress(0, c0, c1, [early[:, :, c0:c1], late[:, :, c0:c1]], nc.vector.tensor_copy, "woven0_0"),
+            compress(1, c0, c1, [head[:, i : i + 1, :] for i in range(PACK)], nc.vector.tensor_copy, "woven1_0"),
+        ]
+        sums = second_product(z)
+        rest_a = keep.tile([P, 2, M - QUARTER], F32, name="rest_a")
+        rest_b = keep.tile([P, 2, M - QUARTER], F32, name="rest_b", tag="woven1_0", align_bytes=64)
+        for i in range(PACK):
+            pick((rest_a, rest_b)[i // 2][:, i % 2, :], sizes1[i], QUARTER, M)
+
+        def later_sums(c0):
+            c1 = c0 + QUARTER
+            r0, r1 = c0 - QUARTER, c1 - QUARTER
+            return second_product([
+                compress(0, c0, c1, [early[:, :, c0:c1], late[:, :, c0:c1]], nc.scalar.copy, "woven0_%d" % c0),
+                compress(1, c0, c1, [rest_a[:, :, r0:r1], rest_b[:, :, r0:r1]], nc.scalar.copy, "woven1_%d" % c0),
+            ])
+
+        for c0 in (0, QUARTER):
+            place_pair(sums, 0, c0, "verdict%d" % c0)
+            following = later_sums(c0 + QUARTER)
+            place_pair(sums, 2, c0, "woven1_%d" % (c0 + QUARTER))
+            sums = following
+        half, last = M // 2, M - QUARTER
+        last_sums = later_sums(last)
+        verdict = keep.tile([P, PACK, half], F32, name="verdict", tag="woven1_%d" % last, align_bytes=64)
+        thicken(verdict[:, :, :QUARTER], sums, 0, PACK, half)
+        place(verdict[:, 0, :QUARTER], 0, half, last)
+        thicken(verdict[:, :, QUARTER:], last_sums, 0, PACK, last)
+        place(verdict[:, 0, QUARTER:], 0, last, M)
+        for i in range(1, PACK):
+            place(verdict[:, i, :], i, half, M)

@@ -23,7 +23,6 @@ K_PASSES = K // PASS
 H_PASSES = H // PASS
 BANK = 512
 QUARTER = 128
-CAST_SPLIT = 88
 
 
 def tile_list_hide_defect_verdicts_kernel(
@@ -32,8 +31,8 @@ def tile_list_hide_defect_verdicts_kernel(
     nc = tc.nc
     with ExitStack() as ctx:
         keep = ctx.enter_context(tc.tile_pool(name="keep", bufs=1))
-        ring = ctx.enter_context(tc.tile_pool(name="ring", bufs=3))
-        hpool = ctx.enter_context(tc.tile_pool(name="hpool", bufs=6))
+        ring = ctx.enter_context(tc.tile_pool(name="ring", bufs=6))
+        hpool = ctx.enter_context(tc.tile_pool(name="hpool", bufs=4))
         psum = ctx.enter_context(tc.psum_pool(name="psum", bufs=8))
 
         strips = keep.tile([P, S // 16], U16, name="strips")
@@ -49,7 +48,7 @@ def tile_list_hide_defect_verdicts_kernel(
         ]
         gains = keep.tile([P, H_PASSES, PACK], F32, name="gains")
         senses = keep.tile([P, H_PASSES, PACK], F32, name="senses")
-        pick_weight = keep.tile([P, M], F32, name="pick_weight")
+        pick_weight = keep.tile([P, M], F32, name="pick_weight", tag="pick_weight", align_bytes=64)
         place_weight = keep.tile([P, M], F32, name="place_weight")
         thickness = keep.tile([P, PACK, M], F32, name="thickness")
         pages = [keep.tile([P, T2], F32, name="page%d" % i) for i in range(PACK)]
@@ -85,12 +84,13 @@ def tile_list_hide_defect_verdicts_kernel(
         load_table(2)
         for a in range(K_PASSES):
             load_w1(0, a)
-        nc.sync.dma_start(pick_weight[:], wgt)
         nc.sync.dma_start(gains[:], gain.rearrange("(b p i) -> p b i", b=H_PASSES, i=PACK))
+        nc.sync.dma_start(pick_weight[:], wgt)
         nc.sync.dma_start(picks[:], offs2)
+        load_w1(1, 0)
+        load_w1(1, 1)
+        load_w1(1, 2)
         nc.sync.dma_start(senses[:], sens.rearrange("(b p i) -> p b i", b=H_PASSES, i=PACK))
-        for a in range(K_PASSES):
-            load_w1(1, a)
         nc.sync.dma_start(thickness[:], thick.rearrange("(p i) m -> p i m", i=PACK))
         nc.sync.dma_start(place_weight[:], wgo)
         nc.sync.dma_start(places[:], offs3)
@@ -114,37 +114,49 @@ def tile_list_hide_defect_verdicts_kernel(
 
         pick_size = keep.tile([P, M], F32, name="pick_size")
 
-        def first_product(b):
-            banks = [[psum.tile([P, BANK], F32, name="bank", tag="bank") for half in range(2)] for i in range(PACK)]
-            for a in range(K_PASSES):
-                grouped = ring.tile([P, PACK, P, PACK], BF16, name="grouped", align_bytes=64)
-                dst = grouped[:].rearrange("p i q j -> p q j i")
-                src = w1_raw[b][a][:].rearrange("p j (q i) -> p q j i", i=PACK)
-                split = P if b == 1 and a < K_PASSES - 1 else CAST_SPLIT
-                nc.vector.tensor_copy(dst[:, :split], src[:, :split])
-                if split < P:
-                    nc.scalar.copy(dst[:, split:], src[:, split:])
-                codes = keep.tile([P, PASS], U32, name="w1_codes%d%d" % (b, a), align_bytes=64)
-                scales = keep.tile([P, PASS], U8, name="w1_scales%d%d" % (b, a), align_bytes=64)
-                nc.vector.quantize_mx(
-                    out=codes[:].bitcast(FP8X4), scales=scales[:], in_=grouped[:].rearrange("p i q j -> p (i q j)")
-                )
-                for i in range(PACK):
-                    for half in range(2):
-                        cols = slice(half * BANK, (half + 1) * BANK)
-                        nc.tensor.matmul_mx(
-                            out=banks[i][half][:],
-                            lhsT=codes[:, i * P : (i + 1) * P].bitcast(FP8X4),
-                            lhsT_scale=scales[:, i * P : (i + 1) * P],
-                            rhs=strip_codes[a][:, cols].bitcast(FP8X4),
-                            rhs_scale=strip_scales[4 * a : P, cols],
-                            start=(a == 0),
-                            stop=(a == K_PASSES - 1),
-                        )
-            return banks
+        def new_banks():
+            return [[psum.tile([P, BANK], F32, name="bank", tag="bank") for half in range(2)] for i in range(PACK)]
+
+        def first_product(banks, b, a, vector_tag=None):
+            if True:
+                src = w1_raw[b][a][:].rearrange("p j (q u v) -> p u q j v", u=2, v=2)
+                scalar_is_free = b == 0 or a == K_PASSES - 1
+                if vector_tag is None:
+                    grouped = [ring.tile([P, 2, P, PACK], BF16, name="grouped", align_bytes=64)[:] for u in range(2)]
+                else:
+                    both = keep.tile([P, 2, 2, P, PACK], BF16, name="both", tag=vector_tag, align_bytes=64)
+                    grouped = [both[:, 0], both[:, 1]]
+                    if scalar_is_free:
+                        grouped[1] = ring.tile([P, 2, P, PACK], BF16, name="grouped", align_bytes=64)[:]
+                for u in range(2):
+                    rounder = nc.scalar.copy if u == 1 and scalar_is_free else nc.vector.tensor_copy
+                    rounder(grouped[u].rearrange("p v q j -> p q j v"), src[:, u])
+                for u in range(2):
+                    codes = keep.tile([P, 2 * P], U32, name="w1_codes%d%d%d" % (b, a, u), align_bytes=64)
+                    scales = keep.tile([P, 2 * P], U8, name="w1_scales%d%d%d" % (b, a, u), align_bytes=64)
+                    nc.vector.quantize_mx(
+                        out=codes[:].bitcast(FP8X4),
+                        scales=scales[:],
+                        in_=grouped[u].rearrange("p v q j -> p (v q j)"),
+                    )
+                    for v in range(2):
+                        for half in range(2):
+                            cols = slice(half * BANK, (half + 1) * BANK)
+                            nc.tensor.matmul_mx(
+                                out=banks[2 * u + v][half][:],
+                                lhsT=codes[:, v * P : (v + 1) * P].bitcast(FP8X4),
+                                lhsT_scale=scales[:, v * P : (v + 1) * P],
+                                rhs=strip_codes[a][:, cols].bitcast(FP8X4),
+                                rhs_scale=strip_scales[4 * a : P, cols],
+                                start=(a == 0),
+                                stop=(a == K_PASSES - 1),
+                            )
 
         def response_size(b, i, banks):
-            size = hpool.tile([P, S], F32, name="size")
+            if b == 0 and i < 2:
+                size = keep.tile([P, S], F32, name="size", tag=("first_size", "pick_weight")[i], align_bytes=64)
+            else:
+                size = hpool.tile([P, S], F32, name="size")
             for half in range(2):
                 nc.scalar.activation(
                     size[:, half * BANK : (half + 1) * BANK], banks[i][half][:], ACT.Abs, scale=gains[:, b, i : i + 1]
@@ -204,19 +216,26 @@ def tile_list_hide_defect_verdicts_kernel(
 
         def place_pair(bank, i0, c0, tag):
             verdict = keep.tile([P, 2, QUARTER], F32, name="verdict", tag=tag, align_bytes=64)
-            thicken(verdict[:], bank, i0, i0 + 2, c0)
+            for i in range(2):
+                thicken(verdict[:, i : i + 1, :], bank, i0 + i, i0 + i + 1, c0)
             for i in range(2):
                 place(verdict[:, i, :], i0 + i, c0, c0 + QUARTER)
 
-        banks0 = first_product(0)
+        banks0 = new_banks()
+        for a in range(K_PASSES):
+            first_product(banks0, 0, a)
         nc.scalar.activation(pick_size[:], pick_weight[:], ACT.Abs)
         sizes0 = [response_size(0, i, banks0) for i in range(PACK)]
-        banks1 = first_product(1)
-        early = keep.tile([P, 1, M], F32, name="early")
-        late = keep.tile([P, PACK - 1, M], F32, name="late", tag="w1_raw12")
+        banks1 = new_banks()
+        first_product(banks1, 1, 0)
+        early = keep.tile([P, 2, M], F32, name="early", tag="w1_raw10")
         pick(early[:, 0, :], sizes0[0], 0, M)
-        for i in range(1, PACK):
-            pick(late[:, i - 1, :], sizes0[i], 0, M)
+        first_product(banks1, 1, 1, "first_size")
+        pick(early[:, 1, :], sizes0[1], 0, M)
+        first_product(banks1, 1, 2, "pick_weight")
+        late = keep.tile([P, 2, M], F32, name="late", tag="w1_raw12")
+        for i in range(2):
+            pick(late[:, i, :], sizes0[2 + i], 0, M)
         head = keep.tile([P, PACK, QUARTER], F32, name="head")
         sizes1 = []
         for i in range(PACK):
@@ -250,9 +269,11 @@ def tile_list_hide_defect_verdicts_kernel(
         half, last = M // 2, M - QUARTER
         last_sums = later_sums(last)
         verdict = keep.tile([P, PACK, half], F32, name="verdict", tag="woven1_%d" % last, align_bytes=64)
-        thicken(verdict[:, :, :QUARTER], sums, 0, PACK, half)
+        thicken(verdict[:, :1, :QUARTER], sums, 0, 1, half)
+        thicken(verdict[:, 1:, :QUARTER], sums, 1, PACK, half)
         place(verdict[:, 0, :QUARTER], 0, half, last)
-        thicken(verdict[:, :, QUARTER:], last_sums, 0, PACK, last)
+        thicken(verdict[:, :1, QUARTER:], last_sums, 0, 1, last)
+        thicken(verdict[:, 1:, QUARTER:], last_sums, 1, PACK, last)
         place(verdict[:, 0, QUARTER:], 0, last, M)
         for i in range(1, PACK):
             place(verdict[:, i, :], i, half, M)

from contextlib import ExitStack

import concourse.mybir as mybir

K, H, N, T, S, M, T2 = 1536, 1024, 512, 4096, 1024, 512, 1024
FLOPS = 2 * K * H * S + 2 * H * N * M

F32 = mybir.dt.float32
BF16 = mybir.dt.bfloat16
I32 = mybir.dt.int32
U32 = mybir.dt.uint32
U16 = mybir.dt.uint16
U8 = mybir.dt.uint8
FP8X4 = mybir.dt.float8_e4m3fn_x4
FP4X4 = mybir.dt.float4_e2m1fn_x4
ALU = mybir.AluOpType
ACT = mybir.ActivationFunctionType

P = 128
PACK = 4
PASS = P * PACK
K_PASSES = K // PASS
H_PASSES = H // PASS
BANK = 512
QUARTER = 128


def tile_list_hide_defect_verdicts_kernel(
    tc, tab_words, tab_scales, offs, w1, gain, offs2, wgt, sens, w2_words, w2_scales, thick, wgo, offs3, out
):
    nc = tc.nc
    with ExitStack() as ctx:
        keep = ctx.enter_context(tc.tile_pool(name="keep", bufs=1))
        ring = ctx.enter_context(tc.tile_pool(name="ring", bufs=6))
        hpool = ctx.enter_context(tc.tile_pool(name="hpool", bufs=4))
        psum = ctx.enter_context(tc.psum_pool(name="psum", bufs=8))

        strips = keep.tile([P, S // 16], U16, name="strips")
        picks = keep.tile([P, M // 16], U16, name="picks")
        places = keep.tile([P, M // 16], U16, name="places")
        table = [keep.tile([P, T], I32, name="table%d" % a) for a in range(K_PASSES)]
        table_scales = keep.tile([P, T], U8, name="table_scales")
        w2_raw = keep.tile([P, H_PASSES, 2 * N], U8, name="w2_raw")
        w2_raw_scales = keep.tile([P, H_PASSES, N], U8, name="w2_raw_scales")
        w1_raw = [
            [keep.tile([P, PACK, PASS], F32, name="w1_raw", tag="w1_raw%d%d" % (b, a)) for a in range(K_PASSES)]
            for b in range(H_PASSES)
        ]
        gains = keep.tile([P, H_PASSES, PACK], F32, name="gains")
        senses = keep.tile([P, H_PASSES, PACK], F32, name="senses")
        pick_weight = keep.tile([P, M], F32, name="pick_weight", tag="pick_weight", align_bytes=64)
        place_weight = keep.tile([P, M], F32, name="place_weight")
        thickness = keep.tile([P, PACK, M], F32, name="thickness")
        pages = [keep.tile([P, T2], F32, name="page%d" % i) for i in range(PACK)]

        nc.vector.memset(table_scales[:].bitcast(I32), 0)
        nc.vector.memset(w2_raw_scales[:].rearrange("p b c -> p (b c)").bitcast(I32), 0)
        ones = keep.tile([P, 1], F32, name="ones")
        one = keep.tile([P, 1], F32, name="one")
        nc.vector.memset(ones[:], 1.0)
        nc.scalar.activation(one[:], ones[:], ACT.Sqrt)

        def load_table(a):
            nc.sync.dma_start(table[a][:], tab_words[a].rearrange("p t i -> p (t i)").bitcast(I32))

        def load_w1(b, a):
            rows = w1[a * PASS : (a + 1) * PASS, b * PASS : (b + 1) * PASS]
            nc.sync.dma_start(w1_raw[b][a][:], rows.rearrange("(p j) c -> p j c", j=PACK))

        nc.sync.dma_start(strips[:], offs)
        load_table(0)
        for quad in range(4):
            nc.sync.dma_start(
                table_scales[32 * quad : 32 * quad + 4 * K_PASSES, :].bitcast(I32),
                tab_scales[:, 4 * quad : 4 * quad + 4, :].bitcast(I32),
            )
        load_table(1)
        nc.sync.dma_start(w2_raw[:].bitcast(I32), w2_words.rearrange("b p c -> p b c").bitcast(I32))
        for quad in range(4):
            nc.sync.dma_start(
                w2_raw_scales[32 * quad : 32 * quad + 4, :, :].bitcast(I32),
                w2_scales[:, 4 * quad : 4 * quad + 4, :].rearrange("b r c -> r b c").bitcast(I32),
            )
        load_table(2)
        for a in range(K_PASSES):
            load_w1(0, a)
        nc.sync.dma_start(gains[:], gain.rearrange("(b p i) -> p b i", b=H_PASSES, i=PACK))
        nc.sync.dma_start(pick_weight[:], wgt)
        nc.sync.dma_start(picks[:], offs2)
        load_w1(1, 0)
        load_w1(1, 1)
        load_w1(1, 2)
        nc.sync.dma_start(senses[:], sens.rearrange("(b p i) -> p b i", b=H_PASSES, i=PACK))
        nc.sync.dma_start(thickness[:], thick.rearrange("(p i) m -> p i m", i=PACK))
        nc.sync.dma_start(place_weight[:], wgo)
        nc.sync.dma_start(places[:], offs3)

        for page in pages:
            nc.vector.memset(page[:], 0.0)

        strip_codes = [keep.tile([P, S], U32, name="strip_codes%d" % a, align_bytes=64) for a in range(K_PASSES)]
        strip_scales = keep.tile([P, S], U8, name="strip_scales", align_bytes=64)
        for a in range(K_PASSES):
            nc.vector.tensor_copy(strip_codes[a][:], table[a][:].bitcast(U32).indirect(strips[:]))
        nc.vector.tensor_copy(strip_scales[:], table_scales[:].indirect(strips[:]))

        w2_codes = keep.tile([P, H_PASSES, PACK, 2 * P], U8, name="w2_codes", align_bytes=64)
        w2_planes = keep.tile([P, H_PASSES, PACK, P], U8, name="w2_planes", align_bytes=64)
        nc.vector.tensor_copy(
            w2_codes[:].rearrange("p b i (q e) -> p b i q e", e=2),
            w2_raw[:].rearrange("p b (q i e) -> p b i q e", i=PACK, e=2),
        )
        nc.vector.tensor_copy(w2_planes[:], w2_raw_scales[:].rearrange("p b (q i) -> p b i q", i=PACK))

        pick_size = keep.tile([P, M], F32, name="pick_size")

        def new_banks():
            return [[psum.tile([P, BANK], F32, name="bank", tag="bank") for half in range(2)] for i in range(PACK)]

        def first_product(banks, b, a, vector_tag=None):
            if True:
                src = w1_raw[b][a][:].rearrange("p j (q u v) -> p u q j v", u=2, v=2)
                scalar_is_free = b == 0 or a == K_PASSES - 1
                if vector_tag is None:
                    grouped = [ring.tile([P, 2, P, PACK], BF16, name="grouped", align_bytes=64)[:] for u in range(2)]
                else:
                    both = keep.tile([P, 2, 2, P, PACK], BF16, name="both", tag=vector_tag, align_bytes=64)
                    grouped = [both[:, 0], both[:, 1]]
                    if scalar_is_free:
                        grouped[1] = ring.tile([P, 2, P, PACK], BF16, name="grouped", align_bytes=64)[:]
                for u in range(2):
                    rounder = nc.scalar.copy if u == 1 and scalar_is_free else nc.vector.tensor_copy
                    rounder(grouped[u].rearrange("p v q j -> p q j v"), src[:, u])
                for u in range(2):
                    codes = keep.tile([P, 2 * P], U32, name="w1_codes%d%d%d" % (b, a, u), align_bytes=64)
                    scales = keep.tile([P, 2 * P], U8, name="w1_scales%d%d%d" % (b, a, u), align_bytes=64)
                    nc.vector.quantize_mx(
                        out=codes[:].bitcast(FP8X4),
                        scales=scales[:],
                        in_=grouped[u].rearrange("p v q j -> p (v q j)"),
                    )
                    for v in range(2):
                        for half in range(2):
                            cols = slice(half * BANK, (half + 1) * BANK)
                            nc.tensor.matmul_mx(
                                out=banks[2 * u + v][half][:],
                                lhsT=codes[:, v * P : (v + 1) * P].bitcast(FP8X4),
                                lhsT_scale=scales[:, v * P : (v + 1) * P],
                                rhs=strip_codes[a][:, cols].bitcast(FP8X4),
                                rhs_scale=strip_scales[4 * a : P, cols],
                                start=(a == 0),
                                stop=(a == K_PASSES - 1),
                            )

        def response_size(b, i, banks):
            if b == 0 and i < 2:
                size = keep.tile([P, S], F32, name="size", tag=("first_size", "pick_weight")[i], align_bytes=64)
            else:
                size = hpool.tile([P, S], F32, name="size")
            for half in range(2):
                nc.scalar.activation(
                    size[:, half * BANK : (half + 1) * BANK], banks[i][half][:], ACT.Abs, scale=gains[:, b, i : i + 1]
                )
            return size

        def pick(dst, size, c0, c1):
            nc.vector.tensor_tensor(dst, size[:].indirect(picks[:, c0 // 16 : c1 // 16]), pick_size[:, c0:c1], ALU.mult)

        def compress(b, c0, c1, groups, weaver, tag):
            width = c1 - c0
            planes = keep.tile([P, PACK, width], BF16, name="planes%d_%d" % (b, c0))
            i = 0
            for group in groups:
                nc.scalar.activation(group, group, ACT.Sqrt, bias=one[:])
                for g in range(group.shape[1]):
                    nc.scalar.activation(planes[:, i, :], group[:, g, :], ACT.Copy, scale=senses[:, b, i : i + 1])
                    i = i + 1
            woven = keep.tile([P, width, PACK], BF16, name="woven", tag=tag, align_bytes=64)
            weaver(
                woven[:].rearrange("p (c e) i -> p c i e", e=4),
                planes[:].rearrange("p i (c e) -> p c i e", e=4),
            )
            codes = keep.tile([P, width], U32, name="z_codes%d_%d" % (b, c0), align_bytes=64)
            scales = keep.tile([P, width], U8, name="z_scales%d_%d" % (b, c0), align_bytes=64)
            nc.vector.quantize_mx(
                out=codes[:].bitcast(FP8X4), scales=scales[:], in_=woven[:].rearrange("p m i -> p (m i)")
            )
            return codes, scales

        def second_product(z):
            bank = psum.tile([P, PACK, QUARTER], F32, name="sums", tag="bank")
            for i in range(PACK):
                for b in range(H_PASSES):
                    nc.tensor.matmul_mx(
                        out=bank[:, i, :],
                        lhsT=w2_codes[:, b, i, :].bitcast(FP4X4),
                        lhsT_scale=w2_planes[:, b, i, :],
                        rhs=z[b][0][:].bitcast(FP8X4),
                        rhs_scale=z[b][1][:],
                        start=(b == 0),
                        stop=(b == H_PASSES - 1),
                    )
            return bank

        rows = out.rearrange("(p i) t -> p i t", i=PACK)

        def thicken(verdict, bank, i0, i1, c0):
            nc.vector.tensor_tensor(verdict, bank[:, i0:i1, :], thickness[:, i0:i1, c0 : c0 + QUARTER], ALU.mult)

        def place(verdict, i, c0, c1):
            nc.vector.tensor_tensor(
                pages[i][:].indirect(places[:, c0 // 16 : c1 // 16]), verdict, place_weight[:, c0:c1], ALU.mult
            )
            if c1 == M:
                nc.sync.dma_start(rows[:, i, :], pages[i][:])

        def place_pair(bank, i0, c0, tag):
            verdict = keep.tile([P, 2, QUARTER], F32, name="verdict", tag=tag, align_bytes=64)
            for i in range(2):
                thicken(verdict[:, i : i + 1, :], bank, i0 + i, i0 + i + 1, c0)
            for i in range(2):
                place(verdict[:, i, :], i0 + i, c0, c0 + QUARTER)

        banks0 = new_banks()
        for a in range(K_PASSES):
            first_product(banks0, 0, a)
        nc.scalar.activation(pick_size[:], pick_weight[:], ACT.Abs)
        sizes0 = [response_size(0, i, banks0) for i in range(PACK)]
        banks1 = new_banks()
        first_product(banks1, 1, 0)
        early = keep.tile([P, 2, M], F32, name="early", tag="w1_raw10")
        pick(early[:, 0, :], sizes0[0], 0, M)
        first_product(banks1, 1, 1, "first_size")
        pick(early[:, 1, :], sizes0[1], 0, M)
        first_product(banks1, 1, 2, "pick_weight")
        late = keep.tile([P, 2, M], F32, name="late", tag="w1_raw12")
        for i in range(2):
            pick(late[:, i, :], sizes0[2 + i], 0, M)
        head = keep.tile([P, PACK, QUARTER], F32, name="head")
        sizes1 = []
        for i in range(PACK):
            sizes1.append(response_size(1, i, banks1))
            pick(head[:, i, :], sizes1[i], 0, QUARTER)

        c0, c1 = 0, QUARTER
        z = [
            compress(0, c0, c1, [early[:, :, c0:c1], late[:, :, c0:c1]], nc.vector.tensor_copy, "woven0_0"),
            compress(1, c0, c1, [head[:, i : i + 1, :] for i in range(PACK)], nc.vector.tensor_copy, "woven1_0"),
        ]
        sums = second_product(z)
        rest_a = keep.tile([P, 2, M - QUARTER], F32, name="rest_a")
        rest_b = keep.tile([P, 2, M - QUARTER], F32, name="rest_b", tag="woven1_0", align_bytes=64)
        for i in range(PACK):
            pick((rest_a, rest_b)[i // 2][:, i % 2, :], sizes1[i], QUARTER, M)

        def later_sums(c0):
            c1 = c0 + QUARTER
            r0, r1 = c0 - QUARTER, c1 - QUARTER
            return second_product([
                compress(0, c0, c1, [early[:, :, c0:c1], late[:, :, c0:c1]], nc.scalar.copy, "woven0_%d" % c0),
                compress(1, c0, c1, [rest_a[:, :, r0:r1], rest_b[:, :, r0:r1]], nc.scalar.copy, "woven1_%d" % c0),
            ])

        for c0 in (0, QUARTER):
            place_pair(sums, 0, c0, "verdict%d" % c0)
            following = later_sums(c0 + QUARTER)
            place_pair(sums, 2, c0, "woven1_%d" % (c0 + QUARTER))
            sums = following
        half, last = M // 2, M - QUARTER
        last_sums = later_sums(last)
        verdict = keep.tile([P, PACK, half], F32, name="verdict", tag="woven1_%d" % last, align_bytes=64)
        thicken(verdict[:, :1, :QUARTER], sums, 0, 1, half)
        thicken(verdict[:, 1:, :QUARTER], sums, 1, PACK, half)
        place(verdict[:, 0, :QUARTER], 0, half, last)
        thicken(verdict[:, :1, QUARTER:], last_sums, 0, 1, last)
        thicken(verdict[:, 1:, QUARTER:], last_sums, 1, PACK, last)
        place(verdict[:, 0, QUARTER:], 0, last, M)
        for i in range(1, PACK):
            place(verdict[:, i, :], i, half, M)
